import numpy as np
import ml_dtypes


def mxq(x, axis, fmt="e4m3"):
    dtype, down = {"e4m3": (ml_dtypes.float8_e4m3fn, 7), "e5m2": (ml_dtypes.float8_e5m2, 14)}[fmt]
    v = np.moveaxis(np.asarray(x, np.float32).astype(ml_dtypes.bfloat16).astype(np.float64), axis, -1)
    blocks = v.reshape(v.shape[:-1] + (-1, 32))
    amax = np.abs(blocks).max(-1, keepdims=True)
    byte = np.maximum(np.where(amax > 0, np.frexp(amax)[1] - 1 + 127, 0) - down, 1)
    scale = np.exp2(byte - 127.0)
    codes = (blocks / scale).astype(np.float32).astype(dtype).astype(np.float64)
    return np.moveaxis((codes * scale).reshape(v.shape), -1, axis)


WIDE = False


def mx_kscale(k):
    if not WIDE:
        return np.ones(k)
    levels = np.array([10, -10, 5, -5, 0])
    if k % 512:
        return np.exp2(np.random.permutation(np.resize(levels, k // 32))).repeat(32)
    a = np.empty((k // 512, 16))
    for p in range(k // 512):
        a[p, :8] = np.random.permutation(np.resize(levels, 8))
        for g in range(8):
            far = levels[np.abs(levels - a[p, g]) >= 10]
            a[p, g + 8] = far[np.random.randint(len(far))]
    return np.exp2(a.ravel()).repeat(32)


def f64(x):
    return np.asarray(x).astype(np.float64)


def striped(idx):
    return np.tile(idx.reshape(-1, 16).T, (8, 1)).astype(np.uint16)


def unstriped(offs):
    return offs[:16].T.reshape(-1).astype(np.int64)


def striped8(idx):
    return np.concatenate([x.reshape(-1, 16).T for x in idx]).astype(np.uint16)


def runs(offs, k):
    lists = np.stack([offs[16 * r : 16 * r + 16].T.reshape(-1) for r in range(8)]).astype(np.int64)
    return lists[np.arange(k) % 512 // 64]


def pack_weight(w):
    k, n = w.shape
    w = f64(np.asarray(w, np.float32).astype(ml_dtypes.bfloat16)).reshape(k // 32, 32, n)
    amax = np.abs(w).max(1)
    byte = np.clip(np.where(amax > 0, np.frexp(amax)[1] - 1 + 127 - 7, 1), 1, 254)
    scaled = (w * np.exp2(127.0 - byte)[:, None, :]).reshape(k, n).astype(np.float32)
    words = np.ascontiguousarray(scaled.reshape(k // 512, 128, 4, n).transpose(0, 1, 3, 2)).astype(ml_dtypes.float8_e4m3fn).view(np.uint8)
    return words, np.ascontiguousarray(byte.astype(np.uint8).reshape(k // 512, 16, n))


def unpack_weight(words, scales):
    g, p, n, _ = words.shape
    vals = np.ascontiguousarray(words).view(ml_dtypes.float8_e4m3fn).astype(np.float64) * np.repeat(np.exp2(scales.astype(np.float64) - 127.0), 8, axis=1)[..., None]
    return vals.transpose(0, 1, 3, 2).reshape(g * 512, n)


def sigmoid(v):
    return 1.0 / (1.0 + np.exp(-np.maximum(v, -700.0)))


K, T, S, H, J, W = 512, 2048, 512, 512, 512, 256


def setup_inputs():
    n = np.random.standard_normal
    s = mx_kscale(K)[:, None]
    u = mx_kscale(S)
    packed_xT = pack_weight(n((K, T)) * s)
    perm = np.stack([np.random.permutation(S) for _ in range(8)])
    return {
        "x_words": packed_xT[0],
        "x_scales": packed_xT[1],
        "w1": (n((K, H)) / np.sqrt(K) / s).astype(np.float32),
        "tab": np.random.uniform(0.4, 1.4, (H, J)).astype(np.float32),
        "ga": (np.random.uniform(0.5, 1.5, (H, 1)) * u[:, None]).astype(np.float32),
        "gb": (np.random.uniform(0.5, 1.5, (H, 1)) / u[:, None]).astype(np.float32),
        "offs": striped(np.random.permutation(T)[:S]),
        "n1": striped8(np.stack([np.random.permutation(S) for _ in range(8)])),
        "n2": striped8(np.stack([np.random.permutation(S) for _ in range(8)])),
        "n3": striped8(np.random.randint(0, J, (8, S))),
        "n4": striped8(np.stack([np.random.permutation(S) for _ in range(8)])),
        "n5": striped8(perm[:, :W]),
        "n6": striped8(perm[:, W:]),
    }


def reference(x_words, x_scales, w1, tab, ga, gb, offs, n1, n2, n3, n4, n5, n6):
    xq = unpack_weight(x_words, x_scales)[:, unstriped(offs)]
    y = mxq(f64(w1), 0, "e4m3").T @ xq
    z = f64(ga) * (y * (sigmoid(y[np.arange(H)[:, None], runs(n1, H)] - (y[np.arange(H)[:, None], runs(n2, H)]))))
    z2 = f64(gb) * (y * (f64(tab)[np.arange(H)[:, None], runs(n3, H)]) - (0.5 * (y[np.arange(H)[:, None], runs(n4, H)])))
    s = 0.0625 * ((mxq(z, 0, "e4m3").T @ mxq(z2, 0, "e4m3")))
    pa = s[np.arange(S)[:, None], runs(n5, S)]
    pb = s[np.arange(S)[:, None], runs(n6, S)]
    rb = np.maximum(0.5 * pa, pb)
    ra = pb - pa
    ds = np.zeros((S, S))
    ds[np.arange(S)[:, None], runs(n5, S)] = ra
    out = ds.copy()
    out[np.arange(S)[:, None], runs(n6, S)] = rb
    return out

@@ -1,0 +1,200 @@
+from contextlib import ExitStack
+
+import concourse.mybir as mybir
+
+K, T, S, H, W = 512, 2048, 512, 512, 256
+FLOPS = 2 * K * H * S + 2 * H * S * S
+
+F32 = mybir.dt.float32
+BF16 = mybir.dt.bfloat16
+I32 = mybir.dt.int32
+U32 = mybir.dt.uint32
+U16 = mybir.dt.uint16
+U8 = mybir.dt.uint8
+FP8X4 = mybir.dt.float8_e4m3fn_x4
+ALU = mybir.AluOpType
+ACT = mybir.ActivationFunctionType
+
+P = 128
+PACK = 4
+Z2_CHUNKS = ((0, 256), (256, 384), (384, 512))
+
+
+def tile_picked_selfcmpkindglift_none_p_kernel(
+    tc, x_words, x_scales, w1, tab, ga, gb, offs, n1, n2, n3, n4, n5, n6, out
+):
+    nc = tc.nc
+    with ExitStack() as ctx:
+        lists = ctx.enter_context(tc.tile_pool(name="lists", bufs=1))
+        sb = ctx.enter_context(tc.tile_pool(name="sb", bufs=1))
+        psum = ctx.enter_context(tc.psum_pool(name="psum", bufs=1))
+
+        def load_list(name, src):
+            tile = lists.tile(list(src.shape), U16, name=name)
+            nc.sync.dma_start(tile[:], src)
+            return tile
+
+        def tiles(name, width, dtype):
+            return [sb.tile([P, width], dtype, name=name + str(t), align_bytes=64) for t in range(PACK)]
+
+        scale_win = sb.tile([P, T], U8, name="scale_win")
+        nc.vector.memset(scale_win[:].bitcast(I32), 0)
+
+        w_raw = sb.tile([P, PACK, H], F32, name="w_raw")
+        nc.sync.dma_start(w_raw[:], w1.rearrange("(p j) h -> p j h", j=PACK))
+        for r in range(4):
+            nc.sync.dma_start(scale_win[r:P:32, :].bitcast(I32), x_scales[0, r:16:4, :].bitcast(I32))
+        offs_t = load_list("offs_t", offs)
+        word_win = sb.tile([P, T], U32, name="word_win")
+        nc.sync.dma_start(word_win[:].bitcast(I32), x_words[0].rearrange("p n r -> p (n r)").bitcast(I32))
+        n2_t = load_list("n2_t", n2)
+        n1_t = load_list("n1_t", n1)
+        gb_t = sb.tile([P, PACK], F32, name="gb_t")
+        nc.sync.dma_start(gb_t[:], gb.rearrange("(p t) o -> p (t o)", t=PACK))
+        ga_t = sb.tile([P, PACK], F32, name="ga_t")
+        nc.sync.dma_start(ga_t[:], ga.rearrange("(p t) o -> p (t o)", t=PACK))
+        n3_t = load_list("n3_t", n3)
+        tab_win = tiles("tab_win", 2 * S, F32)
+        tab_rows = tab.rearrange("(p t) j -> t p j", t=PACK)
+        for t in range(PACK):
+            nc.sync.dma_start(tab_win[t][:, 0:S], tab_rows[t])
+        n4_t = load_list("n4_t", n4)
+        n5_t = load_list("n5_t", n5)
+        n6_t = load_list("n6_t", n6)
+
+        w_in = sb.tile([P, PACK * H], BF16, name="w_in", align_bytes=64)
+        w_dst = w_in[:].rearrange("p (t m j) -> p m j t", t=PACK, j=PACK)
+        w_src = w_raw[:].rearrange("p j (m t) -> p m j t", t=PACK)
+        nc.vector.tensor_copy(w_dst[:, 0:80], w_src[:, 0:80])
+        nc.scalar.copy(w_dst[:, 80:128], w_src[:, 80:128])
+        x_scale = sb.tile([P, S], U8, name="x_scale", align_bytes=64)
+        nc.vector.tensor_copy(x_scale[:], scale_win[:].indirect(offs_t[:]))
+        w_code = sb.tile([P, H], U32, name="w_code", align_bytes=64)
+        w_scale = sb.tile([P, H], U8, name="w_scale", align_bytes=64)
+        nc.vector.quantize_mx(w_code[:].bitcast(FP8X4), w_scale[:], w_in[:])
+
+        half = S // 2
+        x_code = [sb.tile([P, half], U32, name="x_code" + str(h), align_bytes=64) for h in range(2)]
+        y_win = tiles("y_win", 2 * S, F32)
+        banks = {}
+        for h in range(2):
+            nc.vector.tensor_copy(x_code[h][:], word_win[:].indirect(offs_t[:, 16 * h : 16 * (h + 1)]))
+            for pair in range(2):
+                bank = psum.tile([P, 2, half], F32, name="y_bank", tag="bank" + str(2 * h + pair))
+                banks[h, pair] = bank
+                for e in range(2):
+                    t = 2 * pair + e
+                    nc.tensor.matmul_mx(
+                        bank[:, e, :],
+                        lhsT=w_code[:, P * t : P * (t + 1)].bitcast(FP8X4),
+                        lhsT_scale=w_scale[:, P * t : P * (t + 1)],
+                        rhs=x_code[h][:].bitcast(FP8X4),
+                        rhs_scale=x_scale[:, half * h : half * (h + 1)],
+                        start=True,
+                        stop=True,
+                    )
+        for t in range(PACK):
+            for h in range(2):
+                nc.scalar.copy(y_win[t][:, half * h : half * (h + 1)], banks[h, t // 2][:, t % 2, :])
+
+        y_gb = tiles("y_gb", S, F32)
+        y_half = tiles("y_half", S, F32)
+        at_n2 = tiles("at_n2", S, F32)
+        diff = tiles("diff", S, F32)
+        sig = tiles("sig", S, F32)
+        prod = tiles("prod", S, F32)
+        for t in range(PACK):
+            nc.scalar.activation(y_gb[t][:], y_win[t][:, 0:S], ACT.Copy, scale=gb_t[:, t : t + 1])
+        for t in range(PACK):
+            nc.vector.tensor_copy(at_n2[t][:], y_win[t][:].indirect(n2_t[:]))
+        for t in range(PACK):
+            nc.vector.tensor_tensor(diff[t][:], y_win[t][:].indirect(n1_t[:]), at_n2[t][:], ALU.subtract)
+            nc.scalar.activation(sig[t][:], diff[t][:], ACT.Sigmoid)
+        z_rows = sb.tile([P, PACK, S], BF16, name="z_rows", align_bytes=64)
+        for t in range(PACK):
+            nc.vector.tensor_tensor(prod[t][:], tab_win[t][:].indirect(n3_t[:]), y_gb[t][:], ALU.mult)
+            nc.vector.scalar_tensor_tensor(
+                z_rows[:, t, :], y_win[t][:, 0:S], ga_t[:, t : t + 1], sig[t][:], ALU.mult, ALU.mult
+            )
+            nc.scalar.activation(y_half[t][:], y_gb[t][:], ACT.Copy, scale=-0.5)
+        z_in = sb.tile([P, PACK * S], BF16, name="z_in", align_bytes=64)
+        nc.scalar.copy(
+            z_in[:].rearrange("p (u m t) -> p m t u", u=PACK, t=PACK),
+            z_rows[:].rearrange("p t (m u) -> p m t u", u=PACK),
+        )
+        z_code = sb.tile([P, S], U32, name="z_code", align_bytes=64)
+        z_scale = sb.tile([P, S], U8, name="z_scale", align_bytes=64)
+
+        z2 = []
+        for c, (lo, hi) in enumerate(Z2_CHUNKS):
+            n = hi - lo
+            rows = sb.tile([P, PACK, n], F32, name="z2_rows" + str(c), align_bytes=64)
+            for t in range(PACK):
+                nc.vector.tensor_tensor(
+                    rows[:, t, :], y_half[t][:].indirect(n4_t[:, lo // 16 : hi // 16]), prod[t][:, lo:hi], ALU.add
+                )
+            z2_in = sb.tile([P, PACK * n], BF16, name="z2_in" + str(c), align_bytes=64)
+            nc.scalar.copy(
+                z2_in[:].rearrange("p (c i t) -> p c t i", i=4, t=PACK),
+                rows[:].rearrange("p t (c i) -> p c t i", i=4),
+            )
+            z2.append(z2_in)
+        nc.vector.quantize_mx(z_code[:].bitcast(FP8X4), z_scale[:], z_in[:])
+        z2_code, z2_scale = [], []
+        for c, (lo, hi) in enumerate(Z2_CHUNKS):
+            code = sb.tile([P, hi - lo], U32, name="z2_code" + str(c), align_bytes=64)
+            scale = sb.tile([P, hi - lo], U8, name="z2_scale" + str(c), align_bytes=64)
+            nc.vector.quantize_mx(code[:].bitcast(FP8X4), scale[:], z2[c][:])
+            z2_code.append(code)
+            z2_scale.append(scale)
+
+        s_win = tiles("s_win", S, F32)
+        last_lo = Z2_CHUNKS[-1][0]
+        for u in range(PACK):
+            head = psum.tile([P, last_lo], F32, name="s_head", tag="bank" + str(u))
+            tail = psum.tile([P, S - last_lo], F32, name="s_tail", tag="bank" + str(4 + u))
+            for c, (lo, hi) in enumerate(Z2_CHUNKS):
+                nc.tensor.matmul_mx(
+                    head[:, lo:hi] if hi <= last_lo else tail[:],
+                    lhsT=z_code[:, P * u : P * (u + 1)].bitcast(FP8X4),
+                    lhsT_scale=z_scale[:, P * u : P * (u + 1)],
+                    rhs=z2_code[c][:].bitcast(FP8X4),
+                    rhs_scale=z2_scale[c][:],
+                    start=True,
+                    stop=True,
+                )
+            nc.scalar.activation(s_win[u][:, 0:last_lo], head[:], ACT.Copy, scale=0.0625)
+            nc.scalar.activation(s_win[u][:, last_lo:S], tail[:], ACT.Copy, scale=0.0625)
+
+        neg_pa = tiles("neg_pa", W, F32)
+        pb = tiles("pb", W, F32)
+        rb = tiles("rb", W, F32)
+        res = tiles("res", S, F32)
+        out_rows = out.rearrange("(m u) j -> u m j", u=PACK)
+
+        def fetch_b(u):
+            nc.vector.tensor_copy(pb[u][:], s_win[u][:].indirect(n6_t[:]))
+
+        def fetch_a(u):
+            nc.vector.tensor_scalar(neg_pa[u][:], s_win[u][:].indirect(n5_t[:]), -1.0, 0.0, ALU.mult, ALU.add)
+
+        def larger(u):
+            nc.vector.scalar_tensor_tensor(rb[u][:], neg_pa[u][:], -0.5, pb[u][:], ALU.mult, ALU.max)
+
+        def put_a(u):
+            nc.vector.tensor_tensor(res[u][:].indirect(n5_t[:]), pb[u][:], neg_pa[u][:], ALU.add)
+
+        def put_b(u):
+            nc.vector.tensor_copy(res[u][:].indirect(n6_t[:]), rb[u][:])
+            nc.sync.dma_start(out_rows[u], res[u][:])
+
+        fetch_a(0)
+        fetch_b(0)
+        for u in range(PACK):
+            if u + 1 < PACK:
+                fetch_a(u + 1)
+            larger(u)
+            put_a(u)
+            if u + 1 < PACK:
+                fetch_b(u + 1)
+            put_b(u)

@@ -17,7 +17,7 @@ ACT = mybir.ActivationFunctionType
 
 P = 128
 PACK = 4
-Z2_CHUNKS = ((0, 256), (256, 384), (384, 512))
+W_SPLIT = 32
 
 
 def tile_picked_selfcmpkindglift_none_p_kernel(
@@ -40,161 +40,158 @@ def tile_picked_selfcmpkindglift_none_p_kernel(
         scale_win = sb.tile([P, T], U8, name="scale_win")
         nc.vector.memset(scale_win[:].bitcast(I32), 0)
 
+        tab_win = tiles("tab_win", 2 * S, F32)
+        tab_rows = tab.rearrange("(p t) j -> t p j", t=PACK)
+        n3_t = load_list("n3_t", n3)
+        for t in range(PACK - 1):
+            nc.sync.dma_start(tab_win[t][:, 0:S], tab_rows[t])
         w_raw = sb.tile([P, PACK, H], F32, name="w_raw")
         nc.sync.dma_start(w_raw[:], w1.rearrange("(p j) h -> p j h", j=PACK))
         for r in range(4):
             nc.sync.dma_start(scale_win[r:P:32, :].bitcast(I32), x_scales[0, r:16:4, :].bitcast(I32))
         offs_t = load_list("offs_t", offs)
-        word_win = sb.tile([P, T], U32, name="word_win")
-        nc.sync.dma_start(word_win[:].bitcast(I32), x_words[0].rearrange("p n r -> p (n r)").bitcast(I32))
-        n2_t = load_list("n2_t", n2)
-        n1_t = load_list("n1_t", n1)
         gb_t = sb.tile([P, PACK], F32, name="gb_t")
         nc.sync.dma_start(gb_t[:], gb.rearrange("(p t) o -> p (t o)", t=PACK))
+        word_win = sb.tile([P, T], U32, name="word_win")
+        nc.sync.dma_start(word_win[:].bitcast(I32), x_words[0].rearrange("p n r -> p (n r)").bitcast(I32))
+        nc.sync.dma_start(tab_win[PACK - 1][:, 0:S], tab_rows[PACK - 1])
+        n2_t = load_list("n2_t", n2)
         ga_t = sb.tile([P, PACK], F32, name="ga_t")
         nc.sync.dma_start(ga_t[:], ga.rearrange("(p t) o -> p (t o)", t=PACK))
-        n3_t = load_list("n3_t", n3)
-        tab_win = tiles("tab_win", 2 * S, F32)
-        tab_rows = tab.rearrange("(p t) j -> t p j", t=PACK)
-        for t in range(PACK):
-            nc.sync.dma_start(tab_win[t][:, 0:S], tab_rows[t])
         n4_t = load_list("n4_t", n4)
+        n1_t = load_list("n1_t", n1)
         n5_t = load_list("n5_t", n5)
         n6_t = load_list("n6_t", n6)
+
+        tab_at = tiles("tab_at", S, F32)
+        for t in range(PACK - 1):
+            nc.vector.tensor_copy(tab_at[t][:], tab_win[t][:].indirect(n3_t[:]))
 
         w_in = sb.tile([P, PACK * H], BF16, name="w_in", align_bytes=64)
         w_dst = w_in[:].rearrange("p (t m j) -> p m j t", t=PACK, j=PACK)
         w_src = w_raw[:].rearrange("p j (m t) -> p m j t", t=PACK)
-        nc.vector.tensor_copy(w_dst[:, 0:80], w_src[:, 0:80])
-        nc.scalar.copy(w_dst[:, 80:128], w_src[:, 80:128])
+        nc.vector.tensor_copy(w_dst[:, 0:W_SPLIT], w_src[:, 0:W_SPLIT])
+        nc.scalar.copy(w_dst[:, W_SPLIT:P], w_src[:, W_SPLIT:P])
         x_scale = sb.tile([P, S], U8, name="x_scale", align_bytes=64)
         nc.vector.tensor_copy(x_scale[:], scale_win[:].indirect(offs_t[:]))
         w_code = sb.tile([P, H], U32, name="w_code", align_bytes=64)
         w_scale = sb.tile([P, H], U8, name="w_scale", align_bytes=64)
         nc.vector.quantize_mx(w_code[:].bitcast(FP8X4), w_scale[:], w_in[:])
 
-        half = S // 2
-        x_code = [sb.tile([P, half], U32, name="x_code" + str(h), align_bytes=64) for h in range(2)]
-        y_win = tiles("y_win", 2 * S, F32)
-        banks = {}
-        for h in range(2):
-            nc.vector.tensor_copy(x_code[h][:], word_win[:].indirect(offs_t[:, 16 * h : 16 * (h + 1)]))
-            for pair in range(2):
-                bank = psum.tile([P, 2, half], F32, name="y_bank", tag="bank" + str(2 * h + pair))
-                banks[h, pair] = bank
-                for e in range(2):
-                    t = 2 * pair + e
-                    nc.tensor.matmul_mx(
-                        bank[:, e, :],
-                        lhsT=w_code[:, P * t : P * (t + 1)].bitcast(FP8X4),
-                        lhsT_scale=w_scale[:, P * t : P * (t + 1)],
-                        rhs=x_code[h][:].bitcast(FP8X4),
-                        rhs_scale=x_scale[:, half * h : half * (h + 1)],
-                        start=True,
-                        stop=True,
-                    )
-        for t in range(PACK):
-            for h in range(2):
-                nc.scalar.copy(y_win[t][:, half * h : half * (h + 1)], banks[h, t // 2][:, t % 2, :])
+        tab_gb = tiles("tab_gb", S, F32)[: PACK - 1]
+        for t in range(PACK - 1):
+            nc.scalar.activation(tab_gb[t][:], tab_at[t][:], ACT.Copy, scale=gb_t[:, t : t + 1])
+        gb_half = sb.tile([P, PACK], F32, name="gb_half")
+        nc.scalar.activation(gb_half[:], gb_t[:], ACT.Copy, scale=-0.5)
 
-        y_gb = tiles("y_gb", S, F32)
-        y_half = tiles("y_half", S, F32)
+        half = S // 2
+        x_code = sb.tile([P, S], U32, name="x_code", align_bytes=64)
+        for h in range(2):
+            nc.vector.tensor_copy(
+                x_code[:, half * h : half * (h + 1)], word_win[:].indirect(offs_t[:, 16 * h : 16 * (h + 1)])
+            )
+        nc.vector.tensor_copy(tab_at[PACK - 1][:], tab_win[PACK - 1][:].indirect(n3_t[:]))
+        y_win = tiles("y_win", 2 * S, F32)
+        pieces = [(0, 0, half), (0, half, S)] + [(t, 0, S) for t in range(1, PACK)]
+        for b, (t, lo, hi) in enumerate(pieces):
+            bank = psum.tile([P, hi - lo], F32, name="y_bank", tag="bank" + str(b))
+            nc.tensor.matmul_mx(
+                bank[:],
+                lhsT=w_code[:, P * t : P * (t + 1)].bitcast(FP8X4),
+                lhsT_scale=w_scale[:, P * t : P * (t + 1)],
+                rhs=x_code[:, lo:hi].bitcast(FP8X4),
+                rhs_scale=x_scale[:, lo:hi],
+                start=True,
+                stop=True,
+            )
+            nc.scalar.copy(y_win[t][:, lo:hi], bank[:])
+
+        last = PACK - 1
+        y_gb = sb.tile([P, S], F32, name="y_gb")
+        nc.scalar.activation(y_gb[:], y_win[last][:, 0:S], ACT.Copy, scale=gb_t[:, last:PACK])
+        y_half = tiles("y_half", 2 * S, F32)
+        y_ga = sb.tile([P, PACK, S], F32, name="y_ga")
         at_n2 = tiles("at_n2", S, F32)
-        diff = tiles("diff", S, F32)
-        sig = tiles("sig", S, F32)
-        prod = tiles("prod", S, F32)
         for t in range(PACK):
-            nc.scalar.activation(y_gb[t][:], y_win[t][:, 0:S], ACT.Copy, scale=gb_t[:, t : t + 1])
+            nc.scalar.activation(y_half[t][:, 0:S], y_win[t][:, 0:S], ACT.Copy, scale=gb_half[:, t : t + 1])
+        for t in range(PACK):
+            nc.scalar.activation(y_ga[:, t, :], y_win[t][:, 0:S], ACT.Copy, scale=ga_t[:, t : t + 1])
         for t in range(PACK):
             nc.vector.tensor_copy(at_n2[t][:], y_win[t][:].indirect(n2_t[:]))
+        prod = sb.tile([P, PACK, S], F32, name="prod", tag="prod_then_diff")
+        for t in range(last):
+            nc.vector.tensor_tensor(prod[:, t, :], tab_gb[t][:], y_win[t][:, 0:S], ALU.mult)
+        nc.vector.tensor_tensor(prod[:, last, :], tab_at[last][:], y_gb[:], ALU.mult)
+        z2_rows = sb.tile([P, PACK, S], F32, name="z2_rows")
         for t in range(PACK):
-            nc.vector.tensor_tensor(diff[t][:], y_win[t][:].indirect(n1_t[:]), at_n2[t][:], ALU.subtract)
-            nc.scalar.activation(sig[t][:], diff[t][:], ACT.Sigmoid)
-        z_rows = sb.tile([P, PACK, S], BF16, name="z_rows", align_bytes=64)
-        for t in range(PACK):
-            nc.vector.tensor_tensor(prod[t][:], tab_win[t][:].indirect(n3_t[:]), y_gb[t][:], ALU.mult)
-            nc.vector.scalar_tensor_tensor(
-                z_rows[:, t, :], y_win[t][:, 0:S], ga_t[:, t : t + 1], sig[t][:], ALU.mult, ALU.mult
-            )
-            nc.scalar.activation(y_half[t][:], y_gb[t][:], ACT.Copy, scale=-0.5)
-        z_in = sb.tile([P, PACK * S], BF16, name="z_in", align_bytes=64)
+            nc.vector.tensor_tensor(z2_rows[:, t, :], y_half[t][:].indirect(n4_t[:]), prod[:, t, :], ALU.add)
+        z2_in = sb.tile([P, PACK * S], BF16, name="z2_in", align_bytes=64)
         nc.scalar.copy(
-            z_in[:].rearrange("p (u m t) -> p m t u", u=PACK, t=PACK),
-            z_rows[:].rearrange("p t (m u) -> p m t u", u=PACK),
+            z2_in[:].rearrange("p (c i t) -> p c t i", i=4, t=PACK),
+            z2_rows[:].rearrange("p t (c i) -> p c t i", i=4),
         )
-        z_code = sb.tile([P, S], U32, name="z_code", align_bytes=64)
-        z_scale = sb.tile([P, S], U8, name="z_scale", align_bytes=64)
+        diff = sb.tile([P, PACK, S], F32, name="diff", tag="prod_then_diff")
+        sig = sb.tile([P, PACK, S], F32, name="sig")
+        for t in range(PACK):
+            nc.vector.tensor_tensor(diff[:, t, :], y_win[t][:].indirect(n1_t[:]), at_n2[t][:], ALU.subtract)
+            nc.scalar.activation(sig[:, t, :], diff[:, t, :], ACT.Sigmoid)
+        z2_code = sb.tile([P, S], U32, name="z2_code", align_bytes=64)
+        z2_scale = sb.tile([P, S], U8, name="z2_scale", align_bytes=64)
+        nc.vector.quantize_mx(z2_code[:].bitcast(FP8X4), z2_scale[:], z2_in[:])
 
-        z2 = []
-        for c, (lo, hi) in enumerate(Z2_CHUNKS):
-            n = hi - lo
-            rows = sb.tile([P, PACK, n], F32, name="z2_rows" + str(c), align_bytes=64)
-            for t in range(PACK):
-                nc.vector.tensor_tensor(
-                    rows[:, t, :], y_half[t][:].indirect(n4_t[:, lo // 16 : hi // 16]), prod[t][:, lo:hi], ALU.add
-                )
-            z2_in = sb.tile([P, PACK * n], BF16, name="z2_in" + str(c), align_bytes=64)
-            nc.scalar.copy(
-                z2_in[:].rearrange("p (c i t) -> p c t i", i=4, t=PACK),
-                rows[:].rearrange("p t (c i) -> p c t i", i=4),
-            )
-            z2.append(z2_in)
-        nc.vector.quantize_mx(z_code[:].bitcast(FP8X4), z_scale[:], z_in[:])
-        z2_code, z2_scale = [], []
-        for c, (lo, hi) in enumerate(Z2_CHUNKS):
-            code = sb.tile([P, hi - lo], U32, name="z2_code" + str(c), align_bytes=64)
-            scale = sb.tile([P, hi - lo], U8, name="z2_scale" + str(c), align_bytes=64)
-            nc.vector.quantize_mx(code[:].bitcast(FP8X4), scale[:], z2[c][:])
-            z2_code.append(code)
-            z2_scale.append(scale)
-
+        z_in = tiles("z_in", PACK * P, BF16)
+        z_code = tiles("z_code", P, U32)
+        z_scale = tiles("z_scale", P, U8)
         s_win = tiles("s_win", S, F32)
-        last_lo = Z2_CHUNKS[-1][0]
-        for u in range(PACK):
-            head = psum.tile([P, last_lo], F32, name="s_head", tag="bank" + str(u))
-            tail = psum.tile([P, S - last_lo], F32, name="s_tail", tag="bank" + str(4 + u))
-            for c, (lo, hi) in enumerate(Z2_CHUNKS):
-                nc.tensor.matmul_mx(
-                    head[:, lo:hi] if hi <= last_lo else tail[:],
-                    lhsT=z_code[:, P * u : P * (u + 1)].bitcast(FP8X4),
-                    lhsT_scale=z_scale[:, P * u : P * (u + 1)],
-                    rhs=z2_code[c][:].bitcast(FP8X4),
-                    rhs_scale=z2_scale[c][:],
-                    start=True,
-                    stop=True,
-                )
-            nc.scalar.activation(s_win[u][:, 0:last_lo], head[:], ACT.Copy, scale=0.0625)
-            nc.scalar.activation(s_win[u][:, last_lo:S], tail[:], ACT.Copy, scale=0.0625)
+        y_ga_dealt = y_ga[:].rearrange("p t (b u q) -> p u b t q", u=PACK, q=4)
+        sig_dealt = sig[:].rearrange("p t (b u q) -> p u b t q", u=PACK, q=4)
 
-        neg_pa = tiles("neg_pa", W, F32)
+        def gate(u):
+            nc.vector.tensor_tensor(
+                z_in[u][:].rearrange("p (b q t) -> p b t q", q=4, t=PACK), y_ga_dealt[:, u], sig_dealt[:, u], ALU.mult
+            )
+
+        def second_product(u):
+            nc.vector.quantize_mx(z_code[u][:].bitcast(FP8X4), z_scale[u][:], z_in[u][:])
+            bank = psum.tile([P, S], F32, name="s_bank", tag="bank" + str((5 + u) % 8))
+            nc.tensor.matmul_mx(
+                bank[:],
+                lhsT=z_code[u][:].bitcast(FP8X4),
+                lhsT_scale=z_scale[u][:],
+                rhs=z2_code[:].bitcast(FP8X4),
+                rhs_scale=z2_scale[:],
+                start=True,
+                stop=True,
+            )
+            nc.scalar.activation(s_win[u][:], bank[:], ACT.Copy, scale=0.03125)
+
+        for u in (0, 2):
+            gate(u)
+            gate(u + 1)
+            second_product(u)
+            second_product(u + 1)
+
+        neg_pb = tiles("neg_pb", W, F32)
+        gap = tiles("gap", W, F32)
         pb = tiles("pb", W, F32)
-        rb = tiles("rb", W, F32)
+        lift = tiles("lift", W, F32)
+        gap2 = tiles("gap2", W, F32)
         res = tiles("res", S, F32)
-        out_rows = out.rearrange("(m u) j -> u m j", u=PACK)
+        out_rows = out.rearrange("(b u q) j -> u b q j", u=PACK, q=4)
 
-        def fetch_b(u):
-            nc.vector.tensor_copy(pb[u][:], s_win[u][:].indirect(n6_t[:]))
-
-        def fetch_a(u):
-            nc.vector.tensor_scalar(neg_pa[u][:], s_win[u][:].indirect(n5_t[:]), -1.0, 0.0, ALU.mult, ALU.add)
-
-        def larger(u):
-            nc.vector.scalar_tensor_tensor(rb[u][:], neg_pa[u][:], -0.5, pb[u][:], ALU.mult, ALU.max)
-
-        def put_a(u):
-            nc.vector.tensor_tensor(res[u][:].indirect(n5_t[:]), pb[u][:], neg_pa[u][:], ALU.add)
-
-        def put_b(u):
-            nc.vector.tensor_copy(res[u][:].indirect(n6_t[:]), rb[u][:])
-            nc.sync.dma_start(out_rows[u], res[u][:])
-
-        fetch_a(0)
-        fetch_b(0)
-        for u in range(PACK):
-            if u + 1 < PACK:
-                fetch_a(u + 1)
-            larger(u)
-            put_a(u)
-            if u + 1 < PACK:
-                fetch_b(u + 1)
-            put_b(u)
+        for pair in ((0, 1), (2, 3)):
+            for u in pair:
+                nc.vector.tensor_scalar(neg_pb[u][:], s_win[u][:].indirect(n6_t[:]), -2.0, 0.0, ALU.mult, ALU.add)
+            for u in pair:
+                nc.vector.tensor_tensor(gap[u][:], s_win[u][:].indirect(n5_t[:]), neg_pb[u][:], ALU.add)
+        for pair in ((0, 1), (2, 3)):
+            for u in pair:
+                nc.scalar.activation(gap2[u][:], gap[u][:], ACT.Copy, scale=-2.0)
+            for u in pair:
+                nc.scalar.activation(pb[u][:], neg_pb[u][:], ACT.Copy, scale=-1.0)
+                nc.scalar.activation(lift[u][:], gap[u][:], ACT.Relu)
+            for u in pair:
+                nc.vector.tensor_tensor(res[u][:].indirect(n5_t[:]), gap2[u][:], neg_pb[u][:], ALU.add)
+            for u in pair:
+                nc.vector.tensor_tensor(res[u][:].indirect(n6_t[:]), lift[u][:], pb[u][:], ALU.add)
+                nc.sync.dma_start(out_rows[u], res[u][:])

@@ -120,8 +120,8 @@ def tile_picked_selfcmpkindglift_none_p_kernel(
             nc.vector.tensor_copy(at_n2[t][:], y_win[t][:].indirect(n2_t[:]))
         prod = sb.tile([P, PACK, S], F32, name="prod", tag="prod_then_diff")
         for t in range(last):
-            nc.vector.tensor_tensor(prod[:, t, :], tab_gb[t][:], y_win[t][:, 0:S], ALU.mult)
-        nc.vector.tensor_tensor(prod[:, last, :], tab_at[last][:], y_gb[:], ALU.mult)
+            nc.gpsimd.tensor_tensor(prod[:, t, :], tab_gb[t][:], y_win[t][:, 0:S], ALU.mult)
+        nc.gpsimd.tensor_tensor(prod[:, last, :], tab_at[last][:], y_gb[:], ALU.mult)
         z2_rows = sb.tile([P, PACK, S], F32, name="z2_rows")
         for t in range(PACK):
             nc.vector.tensor_tensor(z2_rows[:, t, :], y_half[t][:].indirect(n4_t[:]), prod[:, t, :], ALU.add)

@@ -17,7 +17,8 @@ ACT = mybir.ActivationFunctionType
 
 P = 128
 PACK = 4
-W_SPLIT = 32
+W_SPLIT = 40
+LATE = 64
 
 
 def tile_picked_selfcmpkindglift_none_p_kernel(
@@ -42,18 +43,19 @@ def tile_picked_selfcmpkindglift_none_p_kernel(
 
         tab_win = tiles("tab_win", 2 * S, F32)
         tab_rows = tab.rearrange("(p t) j -> t p j", t=PACK)
+        nc.sync.dma_start(tab_win[0][:, 0:S], tab_rows[0])
         n3_t = load_list("n3_t", n3)
-        for t in range(PACK - 1):
+        for t in range(1, PACK - 1):
             nc.sync.dma_start(tab_win[t][:, 0:S], tab_rows[t])
         w_raw = sb.tile([P, PACK, H], F32, name="w_raw")
         nc.sync.dma_start(w_raw[:], w1.rearrange("(p j) h -> p j h", j=PACK))
         for r in range(4):
             nc.sync.dma_start(scale_win[r:P:32, :].bitcast(I32), x_scales[0, r:16:4, :].bitcast(I32))
         offs_t = load_list("offs_t", offs)
-        gb_t = sb.tile([P, PACK], F32, name="gb_t")
-        nc.sync.dma_start(gb_t[:], gb.rearrange("(p t) o -> p (t o)", t=PACK))
         word_win = sb.tile([P, T], U32, name="word_win")
         nc.sync.dma_start(word_win[:].bitcast(I32), x_words[0].rearrange("p n r -> p (n r)").bitcast(I32))
+        gb_t = sb.tile([P, PACK], F32, name="gb_t")
+        nc.sync.dma_start(gb_t[:], gb.rearrange("(p t) o -> p (t o)", t=PACK))
         nc.sync.dma_start(tab_win[PACK - 1][:, 0:S], tab_rows[PACK - 1])
         n2_t = load_list("n2_t", n2)
         ga_t = sb.tile([P, PACK], F32, name="ga_t")
@@ -105,10 +107,9 @@ def tile_picked_selfcmpkindglift_none_p_kernel(
                 stop=True,
             )
             nc.scalar.copy(y_win[t][:, lo:hi], bank[:])
+        y_last_bank = bank
 
         last = PACK - 1
-        y_gb = sb.tile([P, S], F32, name="y_gb")
-        nc.scalar.activation(y_gb[:], y_win[last][:, 0:S], ACT.Copy, scale=gb_t[:, last:PACK])
         y_half = tiles("y_half", 2 * S, F32)
         y_ga = sb.tile([P, PACK, S], F32, name="y_ga")
         at_n2 = tiles("at_n2", S, F32)
@@ -121,7 +122,9 @@ def tile_picked_selfcmpkindglift_none_p_kernel(
         prod = sb.tile([P, PACK, S], F32, name="prod", tag="prod_then_diff")
         for t in range(last):
             nc.gpsimd.tensor_tensor(prod[:, t, :], tab_gb[t][:], y_win[t][:, 0:S], ALU.mult)
-        nc.gpsimd.tensor_tensor(prod[:, last, :], tab_at[last][:], y_gb[:], ALU.mult)
+        nc.vector.scalar_tensor_tensor(
+            prod[:, last, :], y_last_bank[:], gb_t[:, last:PACK], tab_at[last][:], ALU.mult, ALU.mult
+        )
         z2_rows = sb.tile([P, PACK, S], F32, name="z2_rows")
         for t in range(PACK):
             nc.vector.tensor_tensor(z2_rows[:, t, :], y_half[t][:].indirect(n4_t[:]), prod[:, t, :], ALU.add)
@@ -163,13 +166,22 @@ def tile_picked_selfcmpkindglift_none_p_kernel(
                 start=True,
                 stop=True,
             )
-            nc.scalar.activation(s_win[u][:], bank[:], ACT.Copy, scale=0.03125)
+            return bank
 
-        for u in (0, 2):
-            gate(u)
-            gate(u + 1)
-            second_product(u)
-            second_product(u + 1)
+        def empty(u, bank, lo, hi):
+            nc.scalar.activation(s_win[u][:, lo:hi], bank[:, lo:hi], ACT.Copy, scale=0.03125)
+
+        gate(0)
+        gate(1)
+        for u in (0, 1):
+            empty(u, second_product(u), 0, S)
+        gate(2)
+        gate(3)
+        bank2 = second_product(2)
+        bank3 = second_product(3)
+        empty(2, bank2, 0, S - LATE)
+        empty(3, bank3, 0, S)
+        empty(2, bank2, S - LATE, S)
 
         neg_pb = tiles("neg_pb", W, F32)
         gap = tiles("gap", W, F32)
@@ -179,12 +191,12 @@ def tile_picked_selfcmpkindglift_none_p_kernel(
         res = tiles("res", S, F32)
         out_rows = out.rearrange("(b u q) j -> u b q j", u=PACK, q=4)
 
-        for pair in ((0, 1), (2, 3)):
+        for pair in ((0, 1), (3, 2)):
             for u in pair:
                 nc.vector.tensor_scalar(neg_pb[u][:], s_win[u][:].indirect(n6_t[:]), -2.0, 0.0, ALU.mult, ALU.add)
             for u in pair:
                 nc.vector.tensor_tensor(gap[u][:], s_win[u][:].indirect(n5_t[:]), neg_pb[u][:], ALU.add)
-        for pair in ((0, 1), (2, 3)):
+        for pair in ((0, 1), (3, 2)):
             for u in pair:
                 nc.scalar.activation(gap2[u][:], gap[u][:], ACT.Copy, scale=-2.0)
             for u in pair:

@@ -17,7 +17,7 @@ ACT = mybir.ActivationFunctionType
 
 P = 128
 PACK = 4
-W_SPLIT = 40
+W_SPLIT = 48
 LATE = 64
 
 
@@ -38,7 +38,11 @@ def tile_picked_selfcmpkindglift_none_p_kernel(
         def tiles(name, width, dtype):
             return [sb.tile([P, width], dtype, name=name + str(t), align_bytes=64) for t in range(PACK)]
 
-        scale_win = sb.tile([P, T], U8, name="scale_win")
+        warm = sb.tile([P, 2], F32, name="warm")
+        nc.gpsimd.memset(warm[:, 0:1], 0.0)
+        nc.scalar.activation(warm[:, 1:2], warm[:, 0:1], ACT.Sigmoid)
+
+        scale_win = sb.tile([P, T], U8, name="scale_win", tag="scale_win_then_w_code", align_bytes=64)
         nc.vector.memset(scale_win[:].bitcast(I32), 0)
 
         tab_win = tiles("tab_win", 2 * S, F32)
@@ -47,7 +51,7 @@ def tile_picked_selfcmpkindglift_none_p_kernel(
         n3_t = load_list("n3_t", n3)
         for t in range(1, PACK - 1):
             nc.sync.dma_start(tab_win[t][:, 0:S], tab_rows[t])
-        w_raw = sb.tile([P, PACK, H], F32, name="w_raw")
+        w_raw = sb.tile([P, PACK, H], F32, name="w_raw", tag="w_raw_then_tab_gb")
         nc.sync.dma_start(w_raw[:], w1.rearrange("(p j) h -> p j h", j=PACK))
         for r in range(4):
             nc.sync.dma_start(scale_win[r:P:32, :].bitcast(I32), x_scales[0, r:16:4, :].bitcast(I32))
@@ -65,26 +69,26 @@ def tile_picked_selfcmpkindglift_none_p_kernel(
         n5_t = load_list("n5_t", n5)
         n6_t = load_list("n6_t", n6)
 
-        tab_at = tiles("tab_at", S, F32)
+        tab_at = tiles("tab_at", S, F32)[: PACK - 1]
         for t in range(PACK - 1):
             nc.vector.tensor_copy(tab_at[t][:], tab_win[t][:].indirect(n3_t[:]))
 
-        w_in = sb.tile([P, PACK * H], BF16, name="w_in", align_bytes=64)
+        w_in = sb.tile([P, PACK * H], BF16, name="w_in", tag="w_in_then_tab", align_bytes=64)
         w_dst = w_in[:].rearrange("p (t m j) -> p m j t", t=PACK, j=PACK)
         w_src = w_raw[:].rearrange("p j (m t) -> p m j t", t=PACK)
         nc.vector.tensor_copy(w_dst[:, 0:W_SPLIT], w_src[:, 0:W_SPLIT])
         nc.scalar.copy(w_dst[:, W_SPLIT:P], w_src[:, W_SPLIT:P])
         x_scale = sb.tile([P, S], U8, name="x_scale", align_bytes=64)
         nc.vector.tensor_copy(x_scale[:], scale_win[:].indirect(offs_t[:]))
-        w_code = sb.tile([P, H], U32, name="w_code", align_bytes=64)
+        w_code = sb.tile([P, H], U32, name="w_code", tag="scale_win_then_w_code", align_bytes=64)
         w_scale = sb.tile([P, H], U8, name="w_scale", align_bytes=64)
         nc.vector.quantize_mx(w_code[:].bitcast(FP8X4), w_scale[:], w_in[:])
 
-        tab_gb = tiles("tab_gb", S, F32)[: PACK - 1]
+        tab_gb = sb.tile([P, PACK - 1, S], F32, name="tab_gb", tag="w_raw_then_tab_gb")
         for t in range(PACK - 1):
-            nc.scalar.activation(tab_gb[t][:], tab_at[t][:], ACT.Copy, scale=gb_t[:, t : t + 1])
+            nc.scalar.activation(tab_gb[:, t, :], tab_at[t][:], ACT.Copy, scale=gb_t[:, t : t + 1])
         gb_half = sb.tile([P, PACK], F32, name="gb_half")
-        nc.scalar.activation(gb_half[:], gb_t[:], ACT.Copy, scale=-0.5)
+        nc.gpsimd.tensor_scalar(gb_half[:], gb_t[:], -0.5, 0.0, ALU.mult, ALU.add)
 
         half = S // 2
         x_code = sb.tile([P, S], U32, name="x_code", align_bytes=64)
@@ -92,6 +96,7 @@ def tile_picked_selfcmpkindglift_none_p_kernel(
             nc.vector.tensor_copy(
                 x_code[:, half * h : half * (h + 1)], word_win[:].indirect(offs_t[:, 16 * h : 16 * (h + 1)])
             )
+        tab_at.append(sb.tile([P, S], F32, name="tab_last", tag="w_in_then_tab", align_bytes=64))
         nc.vector.tensor_copy(tab_at[PACK - 1][:], tab_win[PACK - 1][:].indirect(n3_t[:]))
         y_win = tiles("y_win", 2 * S, F32)
         pieces = [(0, 0, half), (0, half, S)] + [(t, 0, S) for t in range(1, PACK)]
@@ -121,7 +126,7 @@ def tile_picked_selfcmpkindglift_none_p_kernel(
             nc.vector.tensor_copy(at_n2[t][:], y_win[t][:].indirect(n2_t[:]))
         prod = sb.tile([P, PACK, S], F32, name="prod", tag="prod_then_diff")
         for t in range(last):
-            nc.gpsimd.tensor_tensor(prod[:, t, :], tab_gb[t][:], y_win[t][:, 0:S], ALU.mult)
+            nc.gpsimd.tensor_tensor(prod[:, t, :], tab_gb[:, t, :], y_win[t][:, 0:S], ALU.mult)
         nc.vector.scalar_tensor_tensor(
             prod[:, last, :], y_last_bank[:], gb_t[:, last:PACK], tab_at[last][:], ALU.mult, ALU.mult
         )
@@ -171,17 +176,15 @@ def tile_picked_selfcmpkindglift_none_p_kernel(
         def empty(u, bank, lo, hi):
             nc.scalar.activation(s_win[u][:, lo:hi], bank[:, lo:hi], ACT.Copy, scale=0.03125)
 
-        gate(0)
-        gate(1)
-        for u in (0, 1):
-            empty(u, second_product(u), 0, S)
-        gate(2)
-        gate(3)
-        bank2 = second_product(2)
-        bank3 = second_product(3)
-        empty(2, bank2, 0, S - LATE)
-        empty(3, bank3, 0, S)
-        empty(2, bank2, S - LATE, S)
+        pairs = ((1, 0), (3, 2))
+        for whole, split in pairs:
+            gate(split)
+            gate(whole)
+            split_bank = second_product(split)
+            whole_bank = second_product(whole)
+            empty(split, split_bank, 0, S - LATE)
+            empty(whole, whole_bank, 0, S)
+            empty(split, split_bank, S - LATE, S)
 
         neg_pb = tiles("neg_pb", W, F32)
         gap = tiles("gap", W, F32)
@@ -191,12 +194,12 @@ def tile_picked_selfcmpkindglift_none_p_kernel(
         res = tiles("res", S, F32)
         out_rows = out.rearrange("(b u q) j -> u b q j", u=PACK, q=4)
 
-        for pair in ((0, 1), (3, 2)):
+        for pair in pairs:
             for u in pair:
                 nc.vector.tensor_scalar(neg_pb[u][:], s_win[u][:].indirect(n6_t[:]), -2.0, 0.0, ALU.mult, ALU.add)
             for u in pair:
                 nc.vector.tensor_tensor(gap[u][:], s_win[u][:].indirect(n5_t[:]), neg_pb[u][:], ALU.add)
-        for pair in ((0, 1), (3, 2)):
+        for pair in pairs:
             for u in pair:
                 nc.scalar.activation(gap2[u][:], gap[u][:], ACT.Copy, scale=-2.0)
             for u in pair:

from contextlib import ExitStack

import concourse.mybir as mybir

K, T, S, H, W = 512, 2048, 512, 512, 256
FLOPS = 2 * K * H * S + 2 * H * S * S

F32 = mybir.dt.float32
BF16 = mybir.dt.bfloat16
I32 = mybir.dt.int32
U32 = mybir.dt.uint32
U16 = mybir.dt.uint16
U8 = mybir.dt.uint8
FP8X4 = mybir.dt.float8_e4m3fn_x4
ALU = mybir.AluOpType
ACT = mybir.ActivationFunctionType

P = 128
PACK = 4
W_SPLIT = 48
LATE = 64


def tile_picked_selfcmpkindglift_none_p_kernel(
    tc, x_words, x_scales, w1, tab, ga, gb, offs, n1, n2, n3, n4, n5, n6, out
):
    nc = tc.nc
    with ExitStack() as ctx:
        lists = ctx.enter_context(tc.tile_pool(name="lists", bufs=1))
        sb = ctx.enter_context(tc.tile_pool(name="sb", bufs=1))
        psum = ctx.enter_context(tc.psum_pool(name="psum", bufs=1))

        def load_list(name, src):
            tile = lists.tile(list(src.shape), U16, name=name)
            nc.sync.dma_start(tile[:], src)
            return tile

        def tiles(name, width, dtype):
            return [sb.tile([P, width], dtype, name=name + str(t), align_bytes=64) for t in range(PACK)]

        warm = sb.tile([P, 2], F32, name="warm")
        nc.gpsimd.memset(warm[:, 0:1], 0.0)
        nc.scalar.activation(warm[:, 1:2], warm[:, 0:1], ACT.Sigmoid)

        scale_win = sb.tile([P, T], U8, name="scale_win", tag="scale_win_then_w_code", align_bytes=64)
        nc.vector.memset(scale_win[:].bitcast(I32), 0)

        tab_win = tiles("tab_win", 2 * S, F32)
        tab_rows = tab.rearrange("(p t) j -> t p j", t=PACK)
        nc.sync.dma_start(tab_win[0][:, 0:S], tab_rows[0])
        n3_t = load_list("n3_t", n3)
        for t in range(1, PACK - 1):
            nc.sync.dma_start(tab_win[t][:, 0:S], tab_rows[t])
        w_raw = sb.tile([P, PACK, H], F32, name="w_raw", tag="w_raw_then_tab_gb")
        nc.sync.dma_start(w_raw[:], w1.rearrange("(p j) h -> p j h", j=PACK))
        for r in range(4):
            nc.sync.dma_start(scale_win[r:P:32, :].bitcast(I32), x_scales[0, r:16:4, :].bitcast(I32))
        offs_t = load_list("offs_t", offs)
        word_win = sb.tile([P, T], U32, name="word_win")
        nc.sync.dma_start(word_win[:].bitcast(I32), x_words[0].rearrange("p n r -> p (n r)").bitcast(I32))
        gb_t = sb.tile([P, PACK], F32, name="gb_t")
        nc.sync.dma_start(gb_t[:], gb.rearrange("(p t) o -> p (t o)", t=PACK))
        nc.sync.dma_start(tab_win[PACK - 1][:, 0:S], tab_rows[PACK - 1])
        n2_t = load_list("n2_t", n2)
        ga_t = sb.tile([P, PACK], F32, name="ga_t")
        nc.sync.dma_start(ga_t[:], ga.rearrange("(p t) o -> p (t o)", t=PACK))
        n4_t = load_list("n4_t", n4)
        n1_t = load_list("n1_t", n1)
        n5_t = load_list("n5_t", n5)
        n6_t = load_list("n6_t", n6)

        tab_at = tiles("tab_at", S, F32)[: PACK - 1]
        for t in range(PACK - 1):
            nc.vector.tensor_copy(tab_at[t][:], tab_win[t][:].indirect(n3_t[:]))

        w_in = sb.tile([P, PACK * H], BF16, name="w_in", tag="w_in_then_tab", align_bytes=64)
        w_dst = w_in[:].rearrange("p (t m j) -> p m j t", t=PACK, j=PACK)
        w_src = w_raw[:].rearrange("p j (m t) -> p m j t", t=PACK)
        nc.vector.tensor_copy(w_dst[:, 0:W_SPLIT], w_src[:, 0:W_SPLIT])
        nc.scalar.copy(w_dst[:, W_SPLIT:P], w_src[:, W_SPLIT:P])
        x_scale = sb.tile([P, S], U8, name="x_scale", align_bytes=64)
        nc.vector.tensor_copy(x_scale[:], scale_win[:].indirect(offs_t[:]))
        w_code = sb.tile([P, H], U32, name="w_code", tag="scale_win_then_w_code", align_bytes=64)
        w_scale = sb.tile([P, H], U8, name="w_scale", align_bytes=64)
        nc.vector.quantize_mx(w_code[:].bitcast(FP8X4), w_scale[:], w_in[:])

        tab_gb = sb.tile([P, PACK - 1, S], F32, name="tab_gb", tag="w_raw_then_tab_gb")
        for t in range(PACK - 1):
            nc.scalar.activation(tab_gb[:, t, :], tab_at[t][:], ACT.Copy, scale=gb_t[:, t : t + 1])
        gb_half = sb.tile([P, PACK], F32, name="gb_half")
        nc.gpsimd.tensor_scalar(gb_half[:], gb_t[:], -0.5, 0.0, ALU.mult, ALU.add)

        half = S // 2
        x_code = sb.tile([P, S], U32, name="x_code", align_bytes=64)
        for h in range(2):
            nc.vector.tensor_copy(
                x_code[:, half * h : half * (h + 1)], word_win[:].indirect(offs_t[:, 16 * h : 16 * (h + 1)])
            )
        tab_at.append(sb.tile([P, S], F32, name="tab_last", tag="w_in_then_tab", align_bytes=64))
        nc.vector.tensor_copy(tab_at[PACK - 1][:], tab_win[PACK - 1][:].indirect(n3_t[:]))
        y_win = tiles("y_win", 2 * S, F32)
        pieces = [(0, 0, half), (0, half, S)] + [(t, 0, S) for t in range(1, PACK)]
        for b, (t, lo, hi) in enumerate(pieces):
            bank = psum.tile([P, hi - lo], F32, name="y_bank", tag="bank" + str(b))
            nc.tensor.matmul_mx(
                bank[:],
                lhsT=w_code[:, P * t : P * (t + 1)].bitcast(FP8X4),
                lhsT_scale=w_scale[:, P * t : P * (t + 1)],
                rhs=x_code[:, lo:hi].bitcast(FP8X4),
                rhs_scale=x_scale[:, lo:hi],
                start=True,
                stop=True,
            )
            nc.scalar.copy(y_win[t][:, lo:hi], bank[:])
        y_last_bank = bank

        last = PACK - 1
        y_half = tiles("y_half", 2 * S, F32)
        y_ga = sb.tile([P, PACK, S], F32, name="y_ga")
        at_n2 = tiles("at_n2", S, F32)
        for t in range(PACK):
            nc.scalar.activation(y_half[t][:, 0:S], y_win[t][:, 0:S], ACT.Copy, scale=gb_half[:, t : t + 1])
        for t in range(PACK):
            nc.scalar.activation(y_ga[:, t, :], y_win[t][:, 0:S], ACT.Copy, scale=ga_t[:, t : t + 1])
        for t in range(PACK):
            nc.vector.tensor_copy(at_n2[t][:], y_win[t][:].indirect(n2_t[:]))
        prod = sb.tile([P, PACK, S], F32, name="prod", tag="prod_then_diff")
        for t in range(last):
            nc.gpsimd.tensor_tensor(prod[:, t, :], tab_gb[:, t, :], y_win[t][:, 0:S], ALU.mult)
        nc.vector.scalar_tensor_tensor(
            prod[:, last, :], y_last_bank[:], gb_t[:, last:PACK], tab_at[last][:], ALU.mult, ALU.mult
        )
        z2_rows = sb.tile([P, PACK, S], F32, name="z2_rows")
        for t in range(PACK):
            nc.vector.tensor_tensor(z2_rows[:, t, :], y_half[t][:].indirect(n4_t[:]), prod[:, t, :], ALU.add)
        z2_in = sb.tile([P, PACK * S], BF16, name="z2_in", align_bytes=64)
        nc.scalar.copy(
            z2_in[:].rearrange("p (c i t) -> p c t i", i=4, t=PACK),
            z2_rows[:].rearrange("p t (c i) -> p c t i", i=4),
        )
        diff = sb.tile([P, PACK, S], F32, name="diff", tag="prod_then_diff")
        sig = sb.tile([P, PACK, S], F32, name="sig")
        for t in range(PACK):
            nc.vector.tensor_tensor(diff[:, t, :], y_win[t][:].indirect(n1_t[:]), at_n2[t][:], ALU.subtract)
            nc.scalar.activation(sig[:, t, :], diff[:, t, :], ACT.Sigmoid)
        z2_code = sb.tile([P, S], U32, name="z2_code", align_bytes=64)
        z2_scale = sb.tile([P, S], U8, name="z2_scale", align_bytes=64)
        nc.vector.quantize_mx(z2_code[:].bitcast(FP8X4), z2_scale[:], z2_in[:])

        z_in = tiles("z_in", PACK * P, BF16)
        z_code = tiles("z_code", P, U32)
        z_scale = tiles("z_scale", P, U8)
        s_win = tiles("s_win", S, F32)
        y_ga_dealt = y_ga[:].rearrange("p t (b u q) -> p u b t q", u=PACK, q=4)
        sig_dealt = sig[:].rearrange("p t (b u q) -> p u b t q", u=PACK, q=4)

        def gate(u):
            nc.vector.tensor_tensor(
                z_in[u][:].rearrange("p (b q t) -> p b t q", q=4, t=PACK), y_ga_dealt[:, u], sig_dealt[:, u], ALU.mult
            )

        def second_product(u):
            nc.vector.quantize_mx(z_code[u][:].bitcast(FP8X4), z_scale[u][:], z_in[u][:])
            bank = psum.tile([P, S], F32, name="s_bank", tag="bank" + str((5 + u) % 8))
            nc.tensor.matmul_mx(
                bank[:],
                lhsT=z_code[u][:].bitcast(FP8X4),
                lhsT_scale=z_scale[u][:],
                rhs=z2_code[:].bitcast(FP8X4),
                rhs_scale=z2_scale[:],
                start=True,
                stop=True,
            )
            return bank

        def empty(u, bank, lo, hi):
            nc.scalar.activation(s_win[u][:, lo:hi], bank[:, lo:hi], ACT.Copy, scale=0.03125)

        pairs = ((1, 0), (3, 2))
        for whole, split in pairs:
            gate(split)
            gate(whole)
            split_bank = second_product(split)
            whole_bank = second_product(whole)
            empty(split, split_bank, 0, S - LATE)
            empty(whole, whole_bank, 0, S)
            empty(split, split_bank, S - LATE, S)

        neg_pb = tiles("neg_pb", W, F32)
        gap = tiles("gap", W, F32)
        pb = tiles("pb", W, F32)
        lift = tiles("lift", W, F32)
        gap2 = tiles("gap2", W, F32)
        res = tiles("res", S, F32)
        out_rows = out.rearrange("(b u q) j -> u b q j", u=PACK, q=4)

        for pair in pairs:
            for u in pair:
                nc.vector.tensor_scalar(neg_pb[u][:], s_win[u][:].indirect(n6_t[:]), -2.0, 0.0, ALU.mult, ALU.add)
            for u in pair:
                nc.vector.tensor_tensor(gap[u][:], s_win[u][:].indirect(n5_t[:]), neg_pb[u][:], ALU.add)
        for pair in pairs:
            for u in pair:
                nc.scalar.activation(gap2[u][:], gap[u][:], ACT.Copy, scale=-2.0)
            for u in pair:
                nc.scalar.activation(pb[u][:], neg_pb[u][:], ACT.Copy, scale=-1.0)
                nc.scalar.activation(lift[u][:], gap[u][:], ACT.Relu)
            for u in pair:
                nc.vector.tensor_tensor(res[u][:].indirect(n5_t[:]), gap2[u][:], neg_pb[u][:], ALU.add)
            for u in pair:
                nc.vector.tensor_tensor(res[u][:].indirect(n6_t[:]), lift[u][:], pb[u][:], ALU.add)
                nc.sync.dma_start(out_rows[u], res[u][:])
